import numpy as np
import ml_dtypes


def mxq(x, axis, fmt="e4m3"):
    dtype, down = {"e4m3": (ml_dtypes.float8_e4m3fn, 7), "e5m2": (ml_dtypes.float8_e5m2, 14)}[fmt]
    v = np.moveaxis(np.asarray(x, np.float32).astype(ml_dtypes.bfloat16).astype(np.float64), axis, -1)
    blocks = v.reshape(v.shape[:-1] + (-1, 32))
    amax = np.abs(blocks).max(-1, keepdims=True)
    byte = np.maximum(np.where(amax > 0, np.frexp(amax)[1] - 1 + 127, 0) - down, 1)
    scale = np.exp2(byte - 127.0)
    codes = (blocks / scale).astype(np.float32).astype(dtype).astype(np.float64)
    return np.moveaxis((codes * scale).reshape(v.shape), -1, axis)


WIDE = False


def mx_kscale(k):
    if not WIDE:
        return np.ones(k)
    levels = np.array([10, -10, 5, -5, 0])
    if k % 512:
        return np.exp2(np.random.permutation(np.resize(levels, k // 32))).repeat(32)
    a = np.empty((k // 512, 16))
    for p in range(k // 512):
        a[p, :8] = np.random.permutation(np.resize(levels, 8))
        for g in range(8):
            far = levels[np.abs(levels - a[p, g]) >= 10]
            a[p, g + 8] = far[np.random.randint(len(far))]
    return np.exp2(a.ravel()).repeat(32)


def f64(x):
    return np.asarray(x).astype(np.float64)


def striped(idx):
    return np.tile(idx.reshape(-1, 16).T, (8, 1)).astype(np.uint16)


def unstriped(offs):
    return offs[:16].T.reshape(-1).astype(np.int64)


E2M1 = np.array([0.0, 0.5, 1.0, 1.5, 2.0, 3.0, 4.0, 6.0, -0.0, -0.5, -1.0, -1.5, -2.0, -3.0, -4.0, -6.0])


def pack_weight(w, fmt):
    k, n = w.shape
    w = f64(np.asarray(w, np.float32).astype(ml_dtypes.bfloat16)).reshape(k // 32, 32, n)
    amax = np.abs(w).max(1)
    if fmt == "e4m3":
        byte = np.frexp(amax)[1] - 1 + 127 - 7
    else:
        mant, ex = np.frexp(amax / 6.0)
        byte = np.where(mant > 0.5, ex, ex - 1) + 127
    byte = np.clip(np.where(amax > 0, byte, 1), 1, 254)
    scaled = (w * np.exp2(127.0 - byte)[:, None, :]).reshape(k, n).astype(np.float32)
    by_word = np.ascontiguousarray(scaled.reshape(k // 512, 128, 4, n).transpose(0, 1, 3, 2))
    if fmt == "e4m3":
        words = by_word.astype(ml_dtypes.float8_e4m3fn).view(np.uint8)
    else:
        c = by_word.astype(ml_dtypes.float4_e2m1fn).view(np.uint8) & 0xF
        words = (c[..., 0::2] | (c[..., 1::2] << 4)).reshape(k // 512, 128, 2 * n)
    return np.ascontiguousarray(words), np.ascontiguousarray(byte.astype(np.uint8).reshape(k // 512, 16, n))


def unpack_weight(words, scales, fmt):
    g, _, n = scales.shape
    words = np.ascontiguousarray(words).reshape(g, 128, n, -1)
    if fmt == "e4m3":
        vals = words.view(ml_dtypes.float8_e4m3fn).astype(np.float64)
    else:
        nib = np.empty((g, 128, n, 4), np.uint8)
        nib[..., 0::2] = words & 0xF
        nib[..., 1::2] = words >> 4
        vals = E2M1[nib]
    vals = vals * np.repeat(np.exp2(scales.astype(np.float64) - 127.0), 8, axis=1)[..., None]
    return vals.transpose(0, 1, 3, 2).reshape(g * 512, n)


def gelu(v):
    return 0.5 * v * (1.0 + np.tanh(np.sqrt(2.0 / np.pi) * (v + 0.044715 * v**3)))


K, T, S, H, T3, S2, T2 = 1024, 4096, 1024, 512, 2048, 512, 2048

def setup_inputs():
    n = np.random.standard_normal
    s = mx_kscale(K)[:, None]
    u = mx_kscale(H)[:, None]
    tab_words, tab_scales = pack_weight(n((K, T)) * s, "e4m3")
    tab2_words, tab2_scales = pack_weight(n((H, T3)) / np.sqrt(H) / u, "e4m3")
    w3_words, w3_scales = pack_weight(0.8 * n((K, H)) / np.sqrt(K) / s, "e2m1")
    return {
        "tab_words": tab_words, "tab_scales": tab_scales,
        "offs": striped(np.random.permutation(T)[:S]),
        "tab2_words": tab2_words, "tab2_scales": tab2_scales,
        "offs2": striped(np.random.permutation(T3)[:S2]),
        "offs3": striped(np.random.permutation(T2)[:S]),
        "w1": (0.9 * n((K, H)) / np.sqrt(K) / s).astype(np.float32),
        "w2": (0.54 * n((K, H)) / np.sqrt(K) / s).astype(np.float32),
        "w3_words": w3_words, "w3_scales": w3_scales,
        "gain": (np.exp(0.3 * n(H)) * u[:, 0]).astype(np.float32),
        "bench": np.exp(0.4 * n(S2)).astype(np.float32),
        "page1": (0.6 * n((S2, T2))).astype(np.float32),
        "wgo": np.exp(0.3 * n((128, S))).astype(np.float32),
    }

def reference(tab_words, tab_scales, offs, tab2_words, tab2_scales, offs2, offs3, w1, w2, w3_words, w3_scales, gain, bench, page1, wgo):
    v = unpack_weight(tab_words, tab_scales, "e4m3")[:, unstriped(offs)]
    v2 = unpack_weight(tab2_words, tab2_scales, "e4m3")[:, unstriped(offs2)]
    w3 = unpack_weight(w3_words, w3_scales, "e2m1")
    nose = np.tanh(mxq(f64(w1), 0, "e4m3").T @ v)
    palate = np.sin(mxq(f64(w2), 0, "e4m3").T @ v)
    f = w3.T @ v
    finish = 0.5 * f * (1.0 + np.tanh(0.7978845608028654 * (f + 0.044715 * f * f * f)))
    h = f64(gain)[:, None] * (nose + palate + finish)
    e = v2.T @ mxq(h, 0, "e4m3")
    score = f64(bench)[:, None] * e
    out = f64(page1).copy()
    out[:, unstriped(offs3)] = np.tile(f64(wgo), (S2 // 128, 1)) * score
    return out

@@ -1,0 +1,250 @@
+from contextlib import ExitStack
+
+import concourse.mybir as mybir
+from concourse.masks import make_identity
+
+K, T, S, H, T3, S2, T2 = 1024, 4096, 1024, 512, 2048, 512, 2048
+FLOPS = 3 * 2 * K * H * S + 2 * H * S2 * S
+
+F32 = mybir.dt.float32
+BF16 = mybir.dt.bfloat16
+I32 = mybir.dt.int32
+U32 = mybir.dt.uint32
+U16 = mybir.dt.uint16
+U8 = mybir.dt.uint8
+FP8X4 = mybir.dt.float8_e4m3fn_x4
+FP4X4 = mybir.dt.float4_e2m1fn_x4
+ACT = mybir.ActivationFunctionType
+MULT = mybir.AluOpType.mult
+
+P = 128
+PACK = 4
+K_PASS = P * PACK
+PASSES = K // K_PASS
+SCALE_ROWS = 16
+QUADS = 4
+PER_COL = 16
+J_TILES = S // P
+CHUNK = 256
+CHUNKS = S // CHUNK
+BLOCKS = S2 // P
+HALF = S // 2
+
+
+def tile_list_medal_flight_scores_kernel(
+    tc, tab_words, tab_scales, offs, tab2_words, tab2_scales, offs2, offs3,
+    w1, w2, w3_words, w3_scales, gain, bench, page1, wgo, out,
+):
+    nc = tc.nc
+    with ExitStack() as ctx:
+        lists = ctx.enter_context(tc.tile_pool(name="lists", bufs=1))
+        keep = ctx.enter_context(tc.tile_pool(name="keep", bufs=1))
+        ring = ctx.enter_context(tc.tile_pool(name="ring", bufs=4))
+        ps1 = ctx.enter_context(tc.psum_pool(name="ps1", bufs=3))
+        psh = ctx.enter_context(tc.psum_pool(name="psh", bufs=3))
+        ps2 = ctx.enter_context(tc.psum_pool(name="ps2", bufs=2))
+
+        def kept(shape, dtype, name, tag=None):
+            return keep.tile(shape, dtype, name=name, tag=tag or name, align_bytes=64)
+
+        idx = lists.tile([P, S // PER_COL], U16, name="idx")
+        idx2 = lists.tile([P, S2 // PER_COL], U16, name="idx2")
+        idx3 = lists.tile([P, S // PER_COL], U16, name="idx3")
+        nc.sync.dma_start(idx[:], offs)
+        nc.sync.dma_start(idx2[:], offs2)
+
+        tab_sc = kept([P, T], U8, "tab_sc")
+        tab2_sc = kept([P, T3], U8, "tab2_sc")
+        w3_plane = kept([P, PASSES, H], U8, "w3_plane")
+        v_low = kept([P, S], U8, "v_low")
+        nc.vector.memset(tab_sc[:].bitcast(I32), 0)
+        nc.vector.memset(w3_plane[:].rearrange("p a c -> p (a c)").bitcast(I32), 0)
+        nc.vector.memset(tab2_sc[:].bitcast(I32), 0)
+        nc.vector.memset(v_low[:].bitcast(I32), 0)
+        for q in range(QUADS):
+            nc.gpsimd.dma_start(
+                tab_sc[32 * q : 32 * q + 8, :].bitcast(I32), tab_scales[:, 4 * q : 4 * q + 4, :].bitcast(I32)
+            )
+        for q in range(QUADS):
+            nc.gpsimd.dma_start(
+                w3_plane[32 * q : 32 * q + 4].bitcast(I32),
+                w3_scales[:, 4 * q : 4 * q + 4, :].rearrange("a r c -> r a c").bitcast(I32),
+            )
+        ident = kept([P, P], F32, "ident")
+        make_identity(nc, ident[:])
+
+        tab = []
+        for a in range(PASSES):
+            tab.append(kept([P, T], I32, f"tab{a}"))
+            nc.sync.dma_start(tab[a][:], tab_words[a].rearrange("p t i -> p (t i)").bitcast(I32))
+        w3_codes = kept([P, PASSES, 2 * H], U8, "w3_codes")
+        nc.sync.dma_start(w3_codes[:].bitcast(I32), w3_words.rearrange("a p c -> p a c").bitcast(I32))
+        raw = {}
+        for name, w in (("w1", w1), ("w2", w2)):
+            for a in range(PASSES):
+                raw[name, a] = kept([P, PACK, H], F32, f"{name}_raw{a}")
+                nc.sync.dma_start(raw[name, a][:], w[a * K_PASS : (a + 1) * K_PASS].rearrange("(p i) r -> p i r", i=PACK))
+        tab2 = kept([P, T3], I32, "tab2")
+        nc.sync.dma_start(tab2[:], tab2_words[0].rearrange("p t i -> p (t i)").bitcast(I32))
+        gain_sb = kept([P, PACK], F32, "gain_sb")
+        nc.sync.dma_start(gain_sb[:], gain.rearrange("(p t) -> p t", t=PACK))
+        bench_sb = kept([P, BLOCKS], F32, "bench_sb")
+        with nc.allow_non_contiguous_dma(reason="one bench value a partition"):
+            nc.sync.dma_start(bench_sb[:], bench.rearrange("(b p) -> p b", p=P))
+        nc.sync.dma_start(idx3[:], offs3)
+        wgo_first = kept([P, CHUNK], F32, "wgo_first")
+        nc.sync.dma_start(wgo_first[:], wgo[:, 0:CHUNK])
+        page = []
+        for b in range(BLOCKS):
+            page.append(kept([P, T2], F32, f"page{b}"))
+            nc.sync.dma_start(page[b][:], page1[b * P : (b + 1) * P])
+        wgo_rest = kept([P, S - CHUNK], F32, "wgo_rest")
+        nc.sync.dma_start(wgo_rest[:], wgo[:, CHUNK:S])
+
+        v_sc = kept([P, S], U8, "v_sc")
+        nc.vector.tensor_copy(v_sc[:], tab_sc[:].indirect(idx[:]))
+        nc.gpsimd.dma_start(v_low[0:100, :].bitcast(I32), v_sc[4:104, :].bitcast(I32))
+        for q in range(QUADS):
+            nc.gpsimd.dma_start(
+                tab2_sc[32 * q + 8 : 32 * q + 12, :].bitcast(I32), tab2_scales[0, 4 * q : 4 * q + 4, :].bitcast(I32)
+            )
+        v_planes = [v_sc[:], v_sc[4:P, :]]
+        v_planes_low = [v_sc[:], v_low[:]]
+
+        v_codes = {}
+        for a in range(PASSES):
+            for half in range(2):
+                v_codes[a, half] = kept([P, HALF], U32, f"v_codes{a}{half}")
+                cols = slice(half * HALF // PER_COL, (half + 1) * HALF // PER_COL)
+                nc.vector.tensor_copy(v_codes[a, half][:], tab[a][:].bitcast(U32).indirect(idx[:, cols]))
+
+        def first_stage(jt, weights, planes, func, dst):
+            acc = ps1.tile([P, H], F32, name="acc")
+            half, j0 = divmod(jt * P, HALF)
+            for a in range(PASSES):
+                codes, plane = weights[a]
+                nc.tensor.matmul_mx(
+                    acc[:],
+                    lhsT=v_codes[a, half][:, j0 : j0 + P].bitcast(FP8X4),
+                    lhsT_scale=planes[a][:, jt * P : (jt + 1) * P],
+                    rhs=codes,
+                    rhs_scale=plane,
+                    start=(a == 0),
+                    stop=(a == PASSES - 1),
+                )
+            nc.scalar.activation(dst[:], acc[:].rearrange("j (p t) -> j t p", t=PACK), func)
+
+        def quantise_weight(name):
+            made = []
+            for a in range(PASSES):
+                grouped = kept([P, H, PACK], BF16, f"{name}_bf{a}")
+                nc.vector.tensor_copy(
+                    grouped[:].rearrange("p (c u) i -> p c i u", u=4),
+                    raw[name, a][:].rearrange("p i (c u) -> p c i u", u=4),
+                )
+                codes = kept([P, H], U32, f"{name}_codes{a}")
+                plane = kept([P, H], U8, f"{name}_plane{a}")
+                nc.vector.quantize_mx(codes[:].bitcast(FP8X4), plane[:], grouped[:].rearrange("p c i -> p (c i)"))
+                made.append((codes[:].bitcast(FP8X4), plane[:]))
+            return made
+
+        w3_mx = [(w3_codes[:, a, :].bitcast(FP4X4), w3_plane[:, a, :]) for a in range(PASSES)]
+        finish = [kept([P, PACK, P], F32, f"finish{jt}") for jt in range(J_TILES)]
+        for jt in range(J_TILES):
+            first_stage(jt, w3_mx, v_planes_low, ACT.Gelu_apprx_tanh, finish[jt])
+        v2_sc = kept([P, S2], U8, "v2_sc")
+        nc.vector.tensor_copy(v2_sc[:], tab2_sc[:].indirect(idx2[:]))
+        w1_mx = quantise_weight("w1")
+        nose = [kept([P, PACK, P], F32, f"nose{jt}") for jt in range(J_TILES)]
+        for jt in range(J_TILES):
+            first_stage(jt, w1_mx, v_planes, ACT.Tanh, nose[jt])
+        w2_mx = quantise_weight("w2")
+        v2_codes = kept([P, S2], U32, "v2_codes")
+        nc.vector.tensor_copy(v2_codes[:], tab2[:].bitcast(U32).indirect(idx2[:]))
+
+        def palate_of(c):
+            made = []
+            for jt in range(2 * c, 2 * c + 2):
+                palate = ring.tile([P, PACK, P], F32, name="palate")
+                first_stage(jt, w2_mx, v_planes, ACT.Sin, palate)
+                made.append(palate)
+            return made
+
+        def summed(jt, palate):
+            bank = psh.tile([P, PACK, P], F32, name="bank")
+            terms = (finish[jt], nose[jt], palate)
+            for n, term in enumerate(terms):
+                for t in range(PACK):
+                    nc.tensor.matmul(
+                        bank[:, t, :], lhsT=term[:, t, :], rhs=ident[:], is_transpose=True,
+                        start=(n == 0 and t == 0), stop=(n == len(terms) - 1 and t == PACK - 1),
+                    )
+            return bank
+
+        h_mx = {}
+
+        def make_h(c, palates):
+            grouped = kept([P, CHUNK, PACK], BF16, f"h_bf{c}")
+            if c == 0:
+                for u in range(2):
+                    bank = summed(2 * c + u, palates[u])
+                    nc.vector.tensor_tensor(
+                        grouped[:, u * P : (u + 1) * P, :],
+                        bank[:].rearrange("p t j -> p j t"),
+                        gain_sb[:].unsqueeze(1).to_broadcast([P, P, PACK]),
+                        MULT,
+                    )
+            else:
+                rows = kept([P, PACK, CHUNK], BF16, f"h_rows{c}", tag=f"shared{c}")
+                for u in range(2):
+                    bank = summed(2 * c + u, palates[u])
+                    for t in range(PACK):
+                        nc.scalar.activation(
+                            rows[:, t, u * P : (u + 1) * P], bank[:, t, :], ACT.Copy, scale=gain_sb[:, t : t + 1]
+                        )
+                nc.scalar.copy(
+                    grouped[:].rearrange("p (c u) t -> p c t u", u=4),
+                    rows[:].rearrange("p t (c u) -> p c t u", u=4),
+                )
+            codes = kept([P, CHUNK], U32, f"h_codes{c}")
+            plane = kept([P, CHUNK], U8, f"h_plane{c}")
+            nc.vector.quantize_mx(codes[:].bitcast(FP8X4), plane[:], grouped[:].rearrange("p j t -> p (j t)"))
+            h_mx[c] = (codes[:].bitcast(FP8X4), plane[:])
+
+        def place(b, chunks, tag=None):
+            width = CHUNK * len(chunks)
+            bank = ps2.tile([P, 2 * CHUNK], F32, name="bank2")
+            for n, c in enumerate(chunks):
+                nc.tensor.matmul_mx(
+                    bank[:, n * CHUNK : (n + 1) * CHUNK],
+                    lhsT=v2_codes[:, b * P : (b + 1) * P].bitcast(FP8X4),
+                    lhsT_scale=v2_sc[8:P, b * P : (b + 1) * P],
+                    rhs=h_mx[c][0],
+                    rhs_scale=h_mx[c][1],
+                    start=True,
+                    stop=True,
+                )
+            score = kept([P, width], F32, f"score{b}_{chunks[0]}", tag=tag)
+            nc.scalar.activation(score[:], bank[:, 0:width], ACT.Copy, scale=bench_sb[:, b : b + 1])
+            j0 = chunks[0] * CHUNK
+            weight = wgo_first[:] if j0 == 0 else wgo_rest[:, j0 - CHUNK : j0 - CHUNK + width]
+            cols = slice(j0 // PER_COL, (j0 + width) // PER_COL)
+            nc.vector.tensor_tensor(page[b][:].indirect(idx3[:, cols]), score[:], weight, MULT)
+            if chunks[-1] == CHUNKS - 1:
+                nc.sync.dma_start(out[b * P : (b + 1) * P], page[b][:])
+
+        pal = {0: palate_of(0), 1: palate_of(1)}
+        make_h(0, pal[0])
+        for c in range(2):
+            for b in range(BLOCKS - 1):
+                place(b, [c])
+            make_h(c + 1, pal[c + 1])
+            place(BLOCKS - 1, [c], tag=f"shared{c + 1}")
+            pal[c + 2] = palate_of(c + 2)
+        place(0, [2])
+        place(1, [2])
+        make_h(3, pal[3])
+        place(2, [2], tag="shared3")
+        for b in range(BLOCKS - 1):
+            place(b, [3])
+        place(3, [2, 3])

@@ -29,6 +29,7 @@ CHUNK = 256
 CHUNKS = S // CHUNK
 BLOCKS = S2 // P
 HALF = S // 2
+RING = 4
 
 
 def tile_list_medal_flight_scores_kernel(
@@ -39,10 +40,11 @@ def tile_list_medal_flight_scores_kernel(
     with ExitStack() as ctx:
         lists = ctx.enter_context(tc.tile_pool(name="lists", bufs=1))
         keep = ctx.enter_context(tc.tile_pool(name="keep", bufs=1))
-        ring = ctx.enter_context(tc.tile_pool(name="ring", bufs=4))
-        ps1 = ctx.enter_context(tc.psum_pool(name="ps1", bufs=3))
-        psh = ctx.enter_context(tc.psum_pool(name="psh", bufs=3))
-        ps2 = ctx.enter_context(tc.psum_pool(name="ps2", bufs=2))
+        ring = ctx.enter_context(tc.tile_pool(name="ring", bufs=6))
+        psum = ctx.enter_context(tc.psum_pool(name="psum", bufs=1))
+
+        def bank_tile(number, shape, name):
+            return psum.tile(shape, F32, name=name, tag=f"bank{number}")
 
         def kept(shape, dtype, name, tag=None):
             return keep.tile(shape, dtype, name=name, tag=tag or name, align_bytes=64)
@@ -51,7 +53,6 @@ def tile_list_medal_flight_scores_kernel(
         idx2 = lists.tile([P, S2 // PER_COL], U16, name="idx2")
         idx3 = lists.tile([P, S // PER_COL], U16, name="idx3")
         nc.sync.dma_start(idx[:], offs)
-        nc.sync.dma_start(idx2[:], offs2)
 
         tab_sc = kept([P, T], U8, "tab_sc")
         tab2_sc = kept([P, T3], U8, "tab2_sc")
@@ -65,20 +66,28 @@ def tile_list_medal_flight_scores_kernel(
             nc.gpsimd.dma_start(
                 tab_sc[32 * q : 32 * q + 8, :].bitcast(I32), tab_scales[:, 4 * q : 4 * q + 4, :].bitcast(I32)
             )
-        for q in range(QUADS):
-            nc.gpsimd.dma_start(
-                w3_plane[32 * q : 32 * q + 4].bitcast(I32),
-                w3_scales[:, 4 * q : 4 * q + 4, :].rearrange("a r c -> r a c").bitcast(I32),
-            )
         ident = kept([P, P], F32, "ident")
         make_identity(nc, ident[:])
 
         tab = []
         for a in range(PASSES):
             tab.append(kept([P, T], I32, f"tab{a}"))
-            nc.sync.dma_start(tab[a][:], tab_words[a].rearrange("p t i -> p (t i)").bitcast(I32))
-        w3_codes = kept([P, PASSES, 2 * H], U8, "w3_codes")
-        nc.sync.dma_start(w3_codes[:].bitcast(I32), w3_words.rearrange("a p c -> p a c").bitcast(I32))
+            words = tab_words[a].rearrange("p t i -> p (t i)").bitcast(I32)
+            for half in range(2):
+                cols = slice(half * T // 2, (half + 1) * T // 2)
+                nc.sync.dma_start(tab[a][:, cols], words[:, cols])
+            if a == 0:
+                nc.sync.dma_start(idx2[:], offs2)
+                nc.sync.dma_start(idx3[:], offs3)
+                gain_sb = kept([P, PACK], F32, "gain_sb")
+                nc.sync.dma_start(gain_sb[:], gain.rearrange("(p t) -> p t", t=PACK))
+                for q in range(QUADS):
+                    nc.sync.dma_start(
+                        w3_plane[32 * q : 32 * q + 4].bitcast(I32),
+                        w3_scales[:, 4 * q : 4 * q + 4, :].rearrange("a r c -> r a c").bitcast(I32),
+                    )
+                w3_codes = kept([P, PASSES, 2 * H], U8, "w3_codes")
+                nc.sync.dma_start(w3_codes[:].bitcast(I32), w3_words.rearrange("a p c -> p a c").bitcast(I32))
         raw = {}
         for name, w in (("w1", w1), ("w2", w2)):
             for a in range(PASSES):
@@ -86,12 +95,13 @@ def tile_list_medal_flight_scores_kernel(
                 nc.sync.dma_start(raw[name, a][:], w[a * K_PASS : (a + 1) * K_PASS].rearrange("(p i) r -> p i r", i=PACK))
         tab2 = kept([P, T3], I32, "tab2")
         nc.sync.dma_start(tab2[:], tab2_words[0].rearrange("p t i -> p (t i)").bitcast(I32))
-        gain_sb = kept([P, PACK], F32, "gain_sb")
-        nc.sync.dma_start(gain_sb[:], gain.rearrange("(p t) -> p t", t=PACK))
+        for q in range(QUADS):
+            nc.sync.dma_start(
+                tab2_sc[32 * q + 8 : 32 * q + 12, :].bitcast(I32), tab2_scales[0, 4 * q : 4 * q + 4, :].bitcast(I32)
+            )
         bench_sb = kept([P, BLOCKS], F32, "bench_sb")
         with nc.allow_non_contiguous_dma(reason="one bench value a partition"):
             nc.sync.dma_start(bench_sb[:], bench.rearrange("(b p) -> p b", p=P))
-        nc.sync.dma_start(idx3[:], offs3)
         wgo_first = kept([P, CHUNK], F32, "wgo_first")
         nc.sync.dma_start(wgo_first[:], wgo[:, 0:CHUNK])
         page = []
@@ -101,78 +111,86 @@ def tile_list_medal_flight_scores_kernel(
         wgo_rest = kept([P, S - CHUNK], F32, "wgo_rest")
         nc.sync.dma_start(wgo_rest[:], wgo[:, CHUNK:S])
 
-        v_sc = kept([P, S], U8, "v_sc")
+        def gather_words(a, tag):
+            codes = kept([P, S], U32, f"v_codes{a}", tag=tag)
+            for half in range(2):
+                cols = slice(half * HALF // PER_COL, (half + 1) * HALF // PER_COL)
+                nc.vector.tensor_copy(
+                    codes[:, half * HALF : (half + 1) * HALF], tab[a][:].bitcast(U32).indirect(idx[:, cols])
+                )
+            return codes
+
+        v_codes = [gather_words(0, None)]
+        v_sc = kept([P, S], U8, "v_sc", tag="tab0")
         nc.vector.tensor_copy(v_sc[:], tab_sc[:].indirect(idx[:]))
         nc.gpsimd.dma_start(v_low[0:100, :].bitcast(I32), v_sc[4:104, :].bitcast(I32))
-        for q in range(QUADS):
-            nc.gpsimd.dma_start(
-                tab2_sc[32 * q + 8 : 32 * q + 12, :].bitcast(I32), tab2_scales[0, 4 * q : 4 * q + 4, :].bitcast(I32)
-            )
         v_planes = [v_sc[:], v_sc[4:P, :]]
         v_planes_low = [v_sc[:], v_low[:]]
+        v_codes.append(gather_words(1, "tab_sc"))
+        w_bf = kept([P, 2 * PASSES * H * PACK], BF16, "w_bf", tag="tab1")
 
-        v_codes = {}
-        for a in range(PASSES):
-            for half in range(2):
-                v_codes[a, half] = kept([P, HALF], U32, f"v_codes{a}{half}")
-                cols = slice(half * HALF // PER_COL, (half + 1) * HALF // PER_COL)
-                nc.vector.tensor_copy(v_codes[a, half][:], tab[a][:].bitcast(U32).indirect(idx[:, cols]))
+        def product_pass(acc, jt, a, weights, planes):
+            nc.tensor.matmul_mx(
+                acc[:],
+                lhsT=v_codes[a][:, jt * P : (jt + 1) * P].bitcast(FP8X4),
+                lhsT_scale=planes[a][:, jt * P : (jt + 1) * P],
+                rhs=weights[a][0],
+                rhs_scale=weights[a][1],
+                start=(a == 0),
+                stop=(a == PASSES - 1),
+            )
 
-        def first_stage(jt, weights, planes, func, dst):
-            acc = ps1.tile([P, H], F32, name="acc")
-            half, j0 = divmod(jt * P, HALF)
-            for a in range(PASSES):
-                codes, plane = weights[a]
-                nc.tensor.matmul_mx(
-                    acc[:],
-                    lhsT=v_codes[a, half][:, j0 : j0 + P].bitcast(FP8X4),
-                    lhsT_scale=planes[a][:, jt * P : (jt + 1) * P],
-                    rhs=codes,
-                    rhs_scale=plane,
-                    start=(a == 0),
-                    stop=(a == PASSES - 1),
-                )
+        def feature(acc, func, dst):
             nc.scalar.activation(dst[:], acc[:].rearrange("j (p t) -> j t p", t=PACK), func)
 
-        def quantise_weight(name):
+        def all_tiles(weights, planes, func, name):
+            made = [kept([P, PACK, P], F32, f"{name}{jt}") for jt in range(J_TILES)]
+            for first in range(0, J_TILES, RING):
+                tiles = range(first, first + RING)
+                accs = {jt: bank_tile(jt % RING, [P, H], f"{name}_acc{jt}") for jt in tiles}
+                for jt in tiles:
+                    product_pass(accs[jt], jt, 0, weights, planes)
+                for jt in tiles:
+                    product_pass(accs[jt], jt, 1, weights, planes)
+                    feature(accs[jt], func, made[jt])
+            return made
+
+        def quantise_weight(name, first):
             made = []
             for a in range(PASSES):
-                grouped = kept([P, H, PACK], BF16, f"{name}_bf{a}")
+                grouped = w_bf[:, (first + a) * H * PACK : (first + a + 1) * H * PACK]
                 nc.vector.tensor_copy(
-                    grouped[:].rearrange("p (c u) i -> p c i u", u=4),
+                    grouped.rearrange("p (c u i) -> p c i u", u=4, i=PACK),
                     raw[name, a][:].rearrange("p i (c u) -> p c i u", u=4),
                 )
                 codes = kept([P, H], U32, f"{name}_codes{a}")
                 plane = kept([P, H], U8, f"{name}_plane{a}")
-                nc.vector.quantize_mx(codes[:].bitcast(FP8X4), plane[:], grouped[:].rearrange("p c i -> p (c i)"))
+                nc.vector.quantize_mx(codes[:].bitcast(FP8X4), plane[:], grouped)
                 made.append((codes[:].bitcast(FP8X4), plane[:]))
             return made
 
         w3_mx = [(w3_codes[:, a, :].bitcast(FP4X4), w3_plane[:, a, :]) for a in range(PASSES)]
-        finish = [kept([P, PACK, P], F32, f"finish{jt}") for jt in range(J_TILES)]
-        for jt in range(J_TILES):
-            first_stage(jt, w3_mx, v_planes_low, ACT.Gelu_apprx_tanh, finish[jt])
-        v2_sc = kept([P, S2], U8, "v2_sc")
-        nc.vector.tensor_copy(v2_sc[:], tab2_sc[:].indirect(idx2[:]))
-        w1_mx = quantise_weight("w1")
-        nose = [kept([P, PACK, P], F32, f"nose{jt}") for jt in range(J_TILES)]
-        for jt in range(J_TILES):
-            first_stage(jt, w1_mx, v_planes, ACT.Tanh, nose[jt])
-        w2_mx = quantise_weight("w2")
-        v2_codes = kept([P, S2], U32, "v2_codes")
+        finish = all_tiles(w3_mx, v_planes_low, ACT.Gelu_apprx_tanh, "finish")
+        w1_mx = quantise_weight("w1", 0)
+        nose = all_tiles(w1_mx, v_planes, ACT.Tanh, "nose")
+        w2_mx = quantise_weight("w2", PASSES)
+        v2_codes = kept([P, S2], U32, "v2_codes", tag="tab1")
         nc.vector.tensor_copy(v2_codes[:], tab2[:].bitcast(U32).indirect(idx2[:]))
+        v2_sc = kept([P, S2], U8, "v2_sc", tag="tab2")
+        nc.vector.tensor_copy(v2_sc[:], tab2_sc[:].indirect(idx2[:]))
 
-        def palate_of(c):
-            made = []
-            for jt in range(2 * c, 2 * c + 2):
-                palate = ring.tile([P, PACK, P], F32, name="palate")
-                first_stage(jt, w2_mx, v_planes, ACT.Sin, palate)
-                made.append(palate)
-            return made
+        palate = {}
 
-        def summed(jt, palate):
-            bank = psh.tile([P, PACK, P], F32, name="bank")
-            terms = (finish[jt], nose[jt], palate)
+        def make_palate(jt):
+            acc = bank_tile(jt % 3, [P, H], f"palate_acc{jt}")
+            for a in range(PASSES):
+                product_pass(acc, jt, a, w2_mx, v_planes)
+            palate[jt] = ring.tile([P, PACK, P], F32, name="palate")
+            feature(acc, ACT.Sin, palate[jt])
+
+        def summed(jt):
+            bank = bank_tile(4 + jt if jt < 2 else 6 + jt % 2, [P, PACK, P], f"sum{jt}")
+            terms = (finish[jt], nose[jt], palate[jt])
             for n, term in enumerate(terms):
                 for t in range(PACK):
                     nc.tensor.matmul(
@@ -181,39 +199,38 @@ def tile_list_medal_flight_scores_kernel(
                     )
             return bank
 
+        h_bf = [kept([P, CHUNK, PACK], BF16, f"h_bf{c}") for c in range(CHUNKS)]
+        h_rows = {}
         h_mx = {}
 
-        def make_h(c, palates):
-            grouped = kept([P, CHUNK, PACK], BF16, f"h_bf{c}")
+        def h_tile(jt):
+            c, u = divmod(jt, 2)
+            bank = summed(jt)
+            dst = h_bf[c][:, u * P : (u + 1) * P, :]
             if c == 0:
-                for u in range(2):
-                    bank = summed(2 * c + u, palates[u])
-                    nc.vector.tensor_tensor(
-                        grouped[:, u * P : (u + 1) * P, :],
-                        bank[:].rearrange("p t j -> p j t"),
-                        gain_sb[:].unsqueeze(1).to_broadcast([P, P, PACK]),
-                        MULT,
-                    )
-            else:
-                rows = kept([P, PACK, CHUNK], BF16, f"h_rows{c}", tag=f"shared{c}")
-                for u in range(2):
-                    bank = summed(2 * c + u, palates[u])
-                    for t in range(PACK):
-                        nc.scalar.activation(
-                            rows[:, t, u * P : (u + 1) * P], bank[:, t, :], ACT.Copy, scale=gain_sb[:, t : t + 1]
-                        )
-                nc.scalar.copy(
-                    grouped[:].rearrange("p (c u) t -> p c t u", u=4),
-                    rows[:].rearrange("p t (c u) -> p c t u", u=4),
+                nc.vector.tensor_tensor(
+                    dst, bank[:].rearrange("p t j -> p j t"), gain_sb[:].unsqueeze(1).to_broadcast([P, P, PACK]), MULT
                 )
+                return
+            if u == 0:
+                h_rows[c] = kept([P, 2, PACK, P], BF16, f"h_rows{c}", tag=f"shared{c}")
+            rows = h_rows[c][:, u]
+            for t in range(PACK):
+                nc.scalar.activation(rows[:, t, :], bank[:, t, :], ACT.Copy, scale=gain_sb[:, t : t + 1])
+            nc.scalar.copy(dst.rearrange("p (c u) t -> p c t u", u=4), rows.rearrange("p t (c u) -> p c t u", u=4))
+
+        def quantise_h(c):
             codes = kept([P, CHUNK], U32, f"h_codes{c}")
             plane = kept([P, CHUNK], U8, f"h_plane{c}")
-            nc.vector.quantize_mx(codes[:].bitcast(FP8X4), plane[:], grouped[:].rearrange("p j t -> p (j t)"))
+            nc.vector.quantize_mx(codes[:].bitcast(FP8X4), plane[:], h_bf[c][:].rearrange("p j t -> p (j t)"))
             h_mx[c] = (codes[:].bitcast(FP8X4), plane[:])
+
+        placed = []
 
         def place(b, chunks, tag=None):
             width = CHUNK * len(chunks)
-            bank = ps2.tile([P, 2 * CHUNK], F32, name="bank2")
+            bank = bank_tile(3 + len(placed) % 3, [P, 2 * CHUNK], f"e{b}_{chunks[0]}")
+            placed.append(b)
             for n, c in enumerate(chunks):
                 nc.tensor.matmul_mx(
                     bank[:, n * CHUNK : (n + 1) * CHUNK],
@@ -225,7 +242,10 @@ def tile_list_medal_flight_scores_kernel(
                     stop=True,
                 )
             score = kept([P, width], F32, f"score{b}_{chunks[0]}", tag=tag)
-            nc.scalar.activation(score[:], bank[:, 0:width], ACT.Copy, scale=bench_sb[:, b : b + 1])
+            if len(placed) == 1:
+                nc.vector.tensor_scalar(score[:], bank[:, 0:width], bench_sb[:, b : b + 1], None, MULT)
+            else:
+                nc.scalar.activation(score[:], bank[:, 0:width], ACT.Copy, scale=bench_sb[:, b : b + 1])
             j0 = chunks[0] * CHUNK
             weight = wgo_first[:] if j0 == 0 else wgo_rest[:, j0 - CHUNK : j0 - CHUNK + width]
             cols = slice(j0 // PER_COL, (j0 + width) // PER_COL)
@@ -233,17 +253,28 @@ def tile_list_medal_flight_scores_kernel(
             if chunks[-1] == CHUNKS - 1:
                 nc.sync.dma_start(out[b * P : (b + 1) * P], page[b][:])
 
-        pal = {0: palate_of(0), 1: palate_of(1)}
-        make_h(0, pal[0])
+        def make_h(c):
+            h_tile(2 * c)
+            h_tile(2 * c + 1)
+            quantise_h(c)
+
+        for jt in range(3):
+            make_palate(jt)
+        h_tile(0)
+        make_palate(3)
+        h_tile(1)
+        quantise_h(0)
         for c in range(2):
             for b in range(BLOCKS - 1):
                 place(b, [c])
-            make_h(c + 1, pal[c + 1])
+            make_h(c + 1)
             place(BLOCKS - 1, [c], tag=f"shared{c + 1}")
-            pal[c + 2] = palate_of(c + 2)
+            if c == 0:
+                for jt in range(4, J_TILES):
+                    make_palate(jt)
         place(0, [2])
         place(1, [2])
-        make_h(3, pal[3])
+        make_h(3)
         place(2, [2], tag="shared3")
         for b in range(BLOCKS - 1):
             place(b, [3])

@@ -46,6 +46,11 @@ def tile_list_medal_flight_scores_kernel(
         def bank_tile(number, shape, name):
             return psum.tile(shape, F32, name=name, tag=f"bank{number}")
 
+        reuse = ctx.enter_context(tc.tile_pool(name="reuse", bufs=1))
+
+        def placed_at(kib, shape, dtype, name):
+            return reuse.tile(shape, dtype, name=name, tag=name, align_bytes=64, offset=int(kib * 1024))
+
         def kept(shape, dtype, name, tag=None):
             return keep.tile(shape, dtype, name=name, tag=tag or name, align_bytes=64)
 
@@ -54,24 +59,28 @@ def tile_list_medal_flight_scores_kernel(
         idx3 = lists.tile([P, S // PER_COL], U16, name="idx3")
         nc.sync.dma_start(idx[:], offs)
 
-        tab_sc = kept([P, T], U8, "tab_sc")
-        tab2_sc = kept([P, T3], U8, "tab2_sc")
+        tab_sc = placed_at(34, [P, T], U8, "tab_sc")
+        tab2_sc = placed_at(72, [P, T3], U8, "tab2_sc")
         w3_plane = kept([P, PASSES, H], U8, "w3_plane")
         v_low = kept([P, S], U8, "v_low")
         nc.vector.memset(tab_sc[:].bitcast(I32), 0)
-        nc.vector.memset(w3_plane[:].rearrange("p a c -> p (a c)").bitcast(I32), 0)
         nc.vector.memset(tab2_sc[:].bitcast(I32), 0)
+        nc.vector.memset(w3_plane[:].rearrange("p a c -> p (a c)").bitcast(I32), 0)
         nc.vector.memset(v_low[:].bitcast(I32), 0)
         for q in range(QUADS):
             nc.gpsimd.dma_start(
                 tab_sc[32 * q : 32 * q + 8, :].bitcast(I32), tab_scales[:, 4 * q : 4 * q + 4, :].bitcast(I32)
+            )
+        for q in range(QUADS):
+            nc.gpsimd.dma_start(
+                tab2_sc[32 * q + 8 : 32 * q + 12, :].bitcast(I32), tab2_scales[0, 4 * q : 4 * q + 4, :].bitcast(I32)
             )
         ident = kept([P, P], F32, "ident")
         make_identity(nc, ident[:])
 
         tab = []
         for a in range(PASSES):
-            tab.append(kept([P, T], I32, f"tab{a}"))
+            tab.append(placed_at(16 * a, [P, T], I32, f"tab{a}"))
             words = tab_words[a].rearrange("p t i -> p (t i)").bitcast(I32)
             for half in range(2):
                 cols = slice(half * T // 2, (half + 1) * T // 2)
@@ -89,30 +98,15 @@ def tile_list_medal_flight_scores_kernel(
                 w3_codes = kept([P, PASSES, 2 * H], U8, "w3_codes")
                 nc.sync.dma_start(w3_codes[:].bitcast(I32), w3_words.rearrange("a p c -> p a c").bitcast(I32))
         raw = {}
-        for name, w in (("w1", w1), ("w2", w2)):
-            for a in range(PASSES):
-                raw[name, a] = kept([P, PACK, H], F32, f"{name}_raw{a}")
-                nc.sync.dma_start(raw[name, a][:], w[a * K_PASS : (a + 1) * K_PASS].rearrange("(p i) r -> p i r", i=PACK))
-        tab2 = kept([P, T3], I32, "tab2")
-        nc.sync.dma_start(tab2[:], tab2_words[0].rearrange("p t i -> p (t i)").bitcast(I32))
-        for q in range(QUADS):
-            nc.sync.dma_start(
-                tab2_sc[32 * q + 8 : 32 * q + 12, :].bitcast(I32), tab2_scales[0, 4 * q : 4 * q + 4, :].bitcast(I32)
-            )
-        bench_sb = kept([P, BLOCKS], F32, "bench_sb")
-        with nc.allow_non_contiguous_dma(reason="one bench value a partition"):
-            nc.sync.dma_start(bench_sb[:], bench.rearrange("(b p) -> p b", p=P))
-        wgo_first = kept([P, CHUNK], F32, "wgo_first")
-        nc.sync.dma_start(wgo_first[:], wgo[:, 0:CHUNK])
-        page = []
-        for b in range(BLOCKS):
-            page.append(kept([P, T2], F32, f"page{b}"))
-            nc.sync.dma_start(page[b][:], page1[b * P : (b + 1) * P])
-        wgo_rest = kept([P, S - CHUNK], F32, "wgo_rest")
-        nc.sync.dma_start(wgo_rest[:], wgo[:, CHUNK:S])
 
-        def gather_words(a, tag):
-            codes = kept([P, S], U32, f"v_codes{a}", tag=tag)
+        def load_weight(name, w, a, kib):
+            raw[name, a] = placed_at(kib, [P, PACK, H], F32, f"{name}_raw{a}")
+            nc.sync.dma_start(raw[name, a][:], w[a * K_PASS : (a + 1) * K_PASS].rearrange("(p i) r -> p i r", i=PACK))
+
+        load_weight("w1", w1, 0, 44)
+        load_weight("w1", w1, 1, 64)
+
+        def gather_words(a, codes):
             for half in range(2):
                 cols = slice(half * HALF // PER_COL, (half + 1) * HALF // PER_COL)
                 nc.vector.tensor_copy(
@@ -120,14 +114,16 @@ def tile_list_medal_flight_scores_kernel(
                 )
             return codes
 
-        v_codes = [gather_words(0, None)]
-        v_sc = kept([P, S], U8, "v_sc", tag="tab0")
+        v_codes = [gather_words(0, kept([P, S], U32, "v_codes0"))]
+        v_sc = placed_at(0, [P, S], U8, "v_sc")
         nc.vector.tensor_copy(v_sc[:], tab_sc[:].indirect(idx[:]))
-        nc.gpsimd.dma_start(v_low[0:100, :].bitcast(I32), v_sc[4:104, :].bitcast(I32))
+        for q in range(QUADS):
+            nc.scalar.dma_start(v_low[32 * q : 32 * q + 4, :].bitcast(I32), v_sc[32 * q + 4 : 32 * q + 8, :].bitcast(I32))
+        load_weight("w2", w2, 0, 36)
         v_planes = [v_sc[:], v_sc[4:P, :]]
         v_planes_low = [v_sc[:], v_low[:]]
-        v_codes.append(gather_words(1, "tab_sc"))
-        w_bf = kept([P, 2 * PASSES * H * PACK], BF16, "w_bf", tag="tab1")
+        v_codes.append(gather_words(1, placed_at(32, [P, S], U32, "v_codes1")))
+        load_weight("w2", w2, 1, 24)
 
         def product_pass(acc, jt, a, weights, planes):
             nc.tensor.matmul_mx(
@@ -155,10 +151,10 @@ def tile_list_medal_flight_scores_kernel(
                     feature(accs[jt], func, made[jt])
             return made
 
-        def quantise_weight(name, first):
+        def quantise_weight(name):
             made = []
             for a in range(PASSES):
-                grouped = w_bf[:, (first + a) * H * PACK : (first + a + 1) * H * PACK]
+                grouped = placed_at(16 + 4 * a, [P, H * PACK], BF16, f"{name}_bf{a}")[:]
                 nc.vector.tensor_copy(
                     grouped.rearrange("p (c u i) -> p c i u", u=4, i=PACK),
                     raw[name, a][:].rearrange("p i (c u) -> p c i u", u=4),
@@ -171,13 +167,33 @@ def tile_list_medal_flight_scores_kernel(
 
         w3_mx = [(w3_codes[:, a, :].bitcast(FP4X4), w3_plane[:, a, :]) for a in range(PASSES)]
         finish = all_tiles(w3_mx, v_planes_low, ACT.Gelu_apprx_tanh, "finish")
-        w1_mx = quantise_weight("w1", 0)
+        w1_mx = quantise_weight("w1")
+        tab2 = placed_at(48, [P, T3], I32, "tab2")
+        nc.sync.dma_start(tab2[:], tab2_words[0].rearrange("p t i -> p (t i)").bitcast(I32))
+        bench_sb = placed_at(44, [P, BLOCKS], F32, "bench_sb")
+        with nc.allow_non_contiguous_dma(reason="one bench value a partition"):
+            nc.sync.dma_start(bench_sb[:], bench.rearrange("(b p) -> p b", p=P))
+        wgo_first = placed_at(45, [P, CHUNK], F32, "wgo_first")
+        nc.sync.dma_start(wgo_first[:], wgo[:, 0:CHUNK])
+        page = {}
+
+        def load_page(b, kib):
+            page[b] = placed_at(kib, [P, T2], F32, f"page{b}")
+            nc.sync.dma_start(page[b][:], page1[b * P : (b + 1) * P])
+
+        load_page(0, 64)
         nose = all_tiles(w1_mx, v_planes, ACT.Tanh, "nose")
-        w2_mx = quantise_weight("w2", PASSES)
-        v2_codes = kept([P, S2], U32, "v2_codes", tag="tab1")
+        w2_mx = quantise_weight("w2")
+        load_page(1, 36)
+        load_page(2, 24)
+        v2_codes = placed_at(20, [P, S2], U32, "v2_codes")
         nc.vector.tensor_copy(v2_codes[:], tab2[:].bitcast(U32).indirect(idx2[:]))
-        v2_sc = kept([P, S2], U8, "v2_sc", tag="tab2")
+        load_page(3, 52)
+        v2_sc = placed_at(48, [P, S2], U8, "v2_sc")
         nc.vector.tensor_copy(v2_sc[:], tab2_sc[:].indirect(idx2[:]))
+
+        wgo_rest = placed_at(72, [P, S - CHUNK], F32, "wgo_rest")
+        nc.sync.dma_start(wgo_rest[:], wgo[:, CHUNK:S])
 
         palate = {}
 

from contextlib import ExitStack

import concourse.mybir as mybir
from concourse.masks import make_identity

K, T, S, H, T3, S2, T2 = 1024, 4096, 1024, 512, 2048, 512, 2048
FLOPS = 3 * 2 * K * H * S + 2 * H * S2 * S

F32 = mybir.dt.float32
BF16 = mybir.dt.bfloat16
I32 = mybir.dt.int32
U32 = mybir.dt.uint32
U16 = mybir.dt.uint16
U8 = mybir.dt.uint8
FP8X4 = mybir.dt.float8_e4m3fn_x4
FP4X4 = mybir.dt.float4_e2m1fn_x4
ACT = mybir.ActivationFunctionType
MULT = mybir.AluOpType.mult

P = 128
PACK = 4
K_PASS = P * PACK
PASSES = K // K_PASS
SCALE_ROWS = 16
QUADS = 4
PER_COL = 16
J_TILES = S // P
CHUNK = 256
CHUNKS = S // CHUNK
BLOCKS = S2 // P
HALF = S // 2
RING = 4


def tile_list_medal_flight_scores_kernel(
    tc, tab_words, tab_scales, offs, tab2_words, tab2_scales, offs2, offs3,
    w1, w2, w3_words, w3_scales, gain, bench, page1, wgo, out,
):
    nc = tc.nc
    with ExitStack() as ctx:
        lists = ctx.enter_context(tc.tile_pool(name="lists", bufs=1))
        keep = ctx.enter_context(tc.tile_pool(name="keep", bufs=1))
        ring = ctx.enter_context(tc.tile_pool(name="ring", bufs=6))
        psum = ctx.enter_context(tc.psum_pool(name="psum", bufs=1))

        def bank_tile(number, shape, name):
            return psum.tile(shape, F32, name=name, tag=f"bank{number}")

        reuse = ctx.enter_context(tc.tile_pool(name="reuse", bufs=1))

        def placed_at(kib, shape, dtype, name):
            return reuse.tile(shape, dtype, name=name, tag=name, align_bytes=64, offset=int(kib * 1024))

        def kept(shape, dtype, name, tag=None):
            return keep.tile(shape, dtype, name=name, tag=tag or name, align_bytes=64)

        idx = lists.tile([P, S // PER_COL], U16, name="idx")
        idx2 = lists.tile([P, S2 // PER_COL], U16, name="idx2")
        idx3 = lists.tile([P, S // PER_COL], U16, name="idx3")
        nc.sync.dma_start(idx[:], offs)

        tab_sc = placed_at(34, [P, T], U8, "tab_sc")
        tab2_sc = placed_at(72, [P, T3], U8, "tab2_sc")
        w3_plane = kept([P, PASSES, H], U8, "w3_plane")
        v_low = kept([P, S], U8, "v_low")
        nc.vector.memset(tab_sc[:].bitcast(I32), 0)
        nc.vector.memset(tab2_sc[:].bitcast(I32), 0)
        nc.vector.memset(w3_plane[:].rearrange("p a c -> p (a c)").bitcast(I32), 0)
        nc.vector.memset(v_low[:].bitcast(I32), 0)
        for q in range(QUADS):
            nc.gpsimd.dma_start(
                tab_sc[32 * q : 32 * q + 8, :].bitcast(I32), tab_scales[:, 4 * q : 4 * q + 4, :].bitcast(I32)
            )
        for q in range(QUADS):
            nc.gpsimd.dma_start(
                tab2_sc[32 * q + 8 : 32 * q + 12, :].bitcast(I32), tab2_scales[0, 4 * q : 4 * q + 4, :].bitcast(I32)
            )
        ident = kept([P, P], F32, "ident")
        make_identity(nc, ident[:])

        tab = []
        for a in range(PASSES):
            tab.append(placed_at(16 * a, [P, T], I32, f"tab{a}"))
            words = tab_words[a].rearrange("p t i -> p (t i)").bitcast(I32)
            for half in range(2):
                cols = slice(half * T // 2, (half + 1) * T // 2)
                nc.sync.dma_start(tab[a][:, cols], words[:, cols])
            if a == 0:
                nc.sync.dma_start(idx2[:], offs2)
                nc.sync.dma_start(idx3[:], offs3)
                gain_sb = kept([P, PACK], F32, "gain_sb")
                nc.sync.dma_start(gain_sb[:], gain.rearrange("(p t) -> p t", t=PACK))
                for q in range(QUADS):
                    nc.sync.dma_start(
                        w3_plane[32 * q : 32 * q + 4].bitcast(I32),
                        w3_scales[:, 4 * q : 4 * q + 4, :].rearrange("a r c -> r a c").bitcast(I32),
                    )
                w3_codes = kept([P, PASSES, 2 * H], U8, "w3_codes")
                nc.sync.dma_start(w3_codes[:].bitcast(I32), w3_words.rearrange("a p c -> p a c").bitcast(I32))
        raw = {}

        def load_weight(name, w, a, kib):
            raw[name, a] = placed_at(kib, [P, PACK, H], F32, f"{name}_raw{a}")
            nc.sync.dma_start(raw[name, a][:], w[a * K_PASS : (a + 1) * K_PASS].rearrange("(p i) r -> p i r", i=PACK))

        load_weight("w1", w1, 0, 44)
        load_weight("w1", w1, 1, 64)

        def gather_words(a, codes):
            for half in range(2):
                cols = slice(half * HALF // PER_COL, (half + 1) * HALF // PER_COL)
                nc.vector.tensor_copy(
                    codes[:, half * HALF : (half + 1) * HALF], tab[a][:].bitcast(U32).indirect(idx[:, cols])
                )
            return codes

        v_codes = [gather_words(0, kept([P, S], U32, "v_codes0"))]
        v_sc = placed_at(0, [P, S], U8, "v_sc")
        nc.vector.tensor_copy(v_sc[:], tab_sc[:].indirect(idx[:]))
        for q in range(QUADS):
            nc.scalar.dma_start(v_low[32 * q : 32 * q + 4, :].bitcast(I32), v_sc[32 * q + 4 : 32 * q + 8, :].bitcast(I32))
        load_weight("w2", w2, 0, 36)
        v_planes = [v_sc[:], v_sc[4:P, :]]
        v_planes_low = [v_sc[:], v_low[:]]
        v_codes.append(gather_words(1, placed_at(32, [P, S], U32, "v_codes1")))
        load_weight("w2", w2, 1, 24)

        def product_pass(acc, jt, a, weights, planes):
            nc.tensor.matmul_mx(
                acc[:],
                lhsT=v_codes[a][:, jt * P : (jt + 1) * P].bitcast(FP8X4),
                lhsT_scale=planes[a][:, jt * P : (jt + 1) * P],
                rhs=weights[a][0],
                rhs_scale=weights[a][1],
                start=(a == 0),
                stop=(a == PASSES - 1),
            )

        def feature(acc, func, dst):
            nc.scalar.activation(dst[:], acc[:].rearrange("j (p t) -> j t p", t=PACK), func)

        def all_tiles(weights, planes, func, name):
            made = [kept([P, PACK, P], F32, f"{name}{jt}") for jt in range(J_TILES)]
            for first in range(0, J_TILES, RING):
                tiles = range(first, first + RING)
                accs = {jt: bank_tile(jt % RING, [P, H], f"{name}_acc{jt}") for jt in tiles}
                for jt in tiles:
                    product_pass(accs[jt], jt, 0, weights, planes)
                for jt in tiles:
                    product_pass(accs[jt], jt, 1, weights, planes)
                    feature(accs[jt], func, made[jt])
            return made

        def quantise_weight(name):
            made = []
            for a in range(PASSES):
                grouped = placed_at(16 + 4 * a, [P, H * PACK], BF16, f"{name}_bf{a}")[:]
                nc.vector.tensor_copy(
                    grouped.rearrange("p (c u i) -> p c i u", u=4, i=PACK),
                    raw[name, a][:].rearrange("p i (c u) -> p c i u", u=4),
                )
                codes = kept([P, H], U32, f"{name}_codes{a}")
                plane = kept([P, H], U8, f"{name}_plane{a}")
                nc.vector.quantize_mx(codes[:].bitcast(FP8X4), plane[:], grouped)
                made.append((codes[:].bitcast(FP8X4), plane[:]))
            return made

        w3_mx = [(w3_codes[:, a, :].bitcast(FP4X4), w3_plane[:, a, :]) for a in range(PASSES)]
        finish = all_tiles(w3_mx, v_planes_low, ACT.Gelu_apprx_tanh, "finish")
        w1_mx = quantise_weight("w1")
        tab2 = placed_at(48, [P, T3], I32, "tab2")
        nc.sync.dma_start(tab2[:], tab2_words[0].rearrange("p t i -> p (t i)").bitcast(I32))
        bench_sb = placed_at(44, [P, BLOCKS], F32, "bench_sb")
        with nc.allow_non_contiguous_dma(reason="one bench value a partition"):
            nc.sync.dma_start(bench_sb[:], bench.rearrange("(b p) -> p b", p=P))
        wgo_first = placed_at(45, [P, CHUNK], F32, "wgo_first")
        nc.sync.dma_start(wgo_first[:], wgo[:, 0:CHUNK])
        page = {}

        def load_page(b, kib):
            page[b] = placed_at(kib, [P, T2], F32, f"page{b}")
            nc.sync.dma_start(page[b][:], page1[b * P : (b + 1) * P])

        load_page(0, 64)
        nose = all_tiles(w1_mx, v_planes, ACT.Tanh, "nose")
        w2_mx = quantise_weight("w2")
        load_page(1, 36)
        load_page(2, 24)
        v2_codes = placed_at(20, [P, S2], U32, "v2_codes")
        nc.vector.tensor_copy(v2_codes[:], tab2[:].bitcast(U32).indirect(idx2[:]))
        load_page(3, 52)
        v2_sc = placed_at(48, [P, S2], U8, "v2_sc")
        nc.vector.tensor_copy(v2_sc[:], tab2_sc[:].indirect(idx2[:]))

        wgo_rest = placed_at(72, [P, S - CHUNK], F32, "wgo_rest")
        nc.sync.dma_start(wgo_rest[:], wgo[:, CHUNK:S])

        palate = {}

        def make_palate(jt):
            acc = bank_tile(jt % 3, [P, H], f"palate_acc{jt}")
            for a in range(PASSES):
                product_pass(acc, jt, a, w2_mx, v_planes)
            palate[jt] = ring.tile([P, PACK, P], F32, name="palate")
            feature(acc, ACT.Sin, palate[jt])

        def summed(jt):
            bank = bank_tile(4 + jt if jt < 2 else 6 + jt % 2, [P, PACK, P], f"sum{jt}")
            terms = (finish[jt], nose[jt], palate[jt])
            for n, term in enumerate(terms):
                for t in range(PACK):
                    nc.tensor.matmul(
                        bank[:, t, :], lhsT=term[:, t, :], rhs=ident[:], is_transpose=True,
                        start=(n == 0 and t == 0), stop=(n == len(terms) - 1 and t == PACK - 1),
                    )
            return bank

        h_bf = [kept([P, CHUNK, PACK], BF16, f"h_bf{c}") for c in range(CHUNKS)]
        h_rows = {}
        h_mx = {}

        def h_tile(jt):
            c, u = divmod(jt, 2)
            bank = summed(jt)
            dst = h_bf[c][:, u * P : (u + 1) * P, :]
            if c == 0:
                nc.vector.tensor_tensor(
                    dst, bank[:].rearrange("p t j -> p j t"), gain_sb[:].unsqueeze(1).to_broadcast([P, P, PACK]), MULT
                )
                return
            if u == 0:
                h_rows[c] = kept([P, 2, PACK, P], BF16, f"h_rows{c}", tag=f"shared{c}")
            rows = h_rows[c][:, u]
            for t in range(PACK):
                nc.scalar.activation(rows[:, t, :], bank[:, t, :], ACT.Copy, scale=gain_sb[:, t : t + 1])
            nc.scalar.copy(dst.rearrange("p (c u) t -> p c t u", u=4), rows.rearrange("p t (c u) -> p c t u", u=4))

        def quantise_h(c):
            codes = kept([P, CHUNK], U32, f"h_codes{c}")
            plane = kept([P, CHUNK], U8, f"h_plane{c}")
            nc.vector.quantize_mx(codes[:].bitcast(FP8X4), plane[:], h_bf[c][:].rearrange("p j t -> p (j t)"))
            h_mx[c] = (codes[:].bitcast(FP8X4), plane[:])

        placed = []

        def place(b, chunks, tag=None):
            width = CHUNK * len(chunks)
            bank = bank_tile(3 + len(placed) % 3, [P, 2 * CHUNK], f"e{b}_{chunks[0]}")
            placed.append(b)
            for n, c in enumerate(chunks):
                nc.tensor.matmul_mx(
                    bank[:, n * CHUNK : (n + 1) * CHUNK],
                    lhsT=v2_codes[:, b * P : (b + 1) * P].bitcast(FP8X4),
                    lhsT_scale=v2_sc[8:P, b * P : (b + 1) * P],
                    rhs=h_mx[c][0],
                    rhs_scale=h_mx[c][1],
                    start=True,
                    stop=True,
                )
            score = kept([P, width], F32, f"score{b}_{chunks[0]}", tag=tag)
            if len(placed) == 1:
                nc.vector.tensor_scalar(score[:], bank[:, 0:width], bench_sb[:, b : b + 1], None, MULT)
            else:
                nc.scalar.activation(score[:], bank[:, 0:width], ACT.Copy, scale=bench_sb[:, b : b + 1])
            j0 = chunks[0] * CHUNK
            weight = wgo_first[:] if j0 == 0 else wgo_rest[:, j0 - CHUNK : j0 - CHUNK + width]
            cols = slice(j0 // PER_COL, (j0 + width) // PER_COL)
            nc.vector.tensor_tensor(page[b][:].indirect(idx3[:, cols]), score[:], weight, MULT)
            if chunks[-1] == CHUNKS - 1:
                nc.sync.dma_start(out[b * P : (b + 1) * P], page[b][:])

        def make_h(c):
            h_tile(2 * c)
            h_tile(2 * c + 1)
            quantise_h(c)

        for jt in range(3):
            make_palate(jt)
        h_tile(0)
        make_palate(3)
        h_tile(1)
        quantise_h(0)
        for c in range(2):
            for b in range(BLOCKS - 1):
                place(b, [c])
            make_h(c + 1)
            place(BLOCKS - 1, [c], tag=f"shared{c + 1}")
            if c == 0:
                for jt in range(4, J_TILES):
                    make_palate(jt)
        place(0, [2])
        place(1, [2])
        make_h(3)
        place(2, [2], tag="shared3")
        for b in range(BLOCKS - 1):
            place(b, [3])
        place(3, [2, 3])
